import numpy as np
import ml_dtypes


def mxq(x, axis, fmt="e4m3"):
    dtype, down = {"e4m3": (ml_dtypes.float8_e4m3fn, 7), "e5m2": (ml_dtypes.float8_e5m2, 14)}[fmt]
    v = np.moveaxis(np.asarray(x, np.float32).astype(ml_dtypes.bfloat16).astype(np.float64), axis, -1)
    blocks = v.reshape(v.shape[:-1] + (-1, 32))
    amax = np.abs(blocks).max(-1, keepdims=True)
    byte = np.maximum(np.where(amax > 0, np.frexp(amax)[1] - 1 + 127, 0) - down, 1)
    scale = np.exp2(byte - 127.0)
    codes = (blocks / scale).astype(np.float32).astype(dtype).astype(np.float64)
    return np.moveaxis((codes * scale).reshape(v.shape), -1, axis)


WIDE = False


def mx_kscale(k):
    if not WIDE:
        return np.ones(k)
    levels = np.array([10, -10, 5, -5, 0])
    if k % 512:
        return np.exp2(np.random.permutation(np.resize(levels, k // 32))).repeat(32)
    a = np.empty((k // 512, 16))
    for p in range(k // 512):
        a[p, :8] = np.random.permutation(np.resize(levels, 8))
        for g in range(8):
            far = levels[np.abs(levels - a[p, g]) >= 10]
            a[p, g + 8] = far[np.random.randint(len(far))]
    return np.exp2(a.ravel()).repeat(32)


def f64(x):
    return np.asarray(x).astype(np.float64)


def striped(idx):
    return np.tile(idx.reshape(-1, 16).T, (8, 1)).astype(np.uint16)


def unstriped(offs):
    return offs[:16].T.reshape(-1).astype(np.int64)


def gelu(v):
    return 0.5 * v * (1.0 + np.tanh(np.sqrt(2.0 / np.pi) * (v + 0.044715 * v**3)))


K, T, E, C, N = 512, 1024, 8, 256, 256


def by_expert(wq, xq):
    return np.concatenate([wq[e].T @ xq[:, e * C:(e + 1) * C] for e in range(E)], axis=1)


def setup_inputs():
    n = np.random.standard_normal
    s = mx_kscale(K)[:, None]
    first = np.random.permutation(np.repeat(np.arange(E), T // E))
    second = (first + 1 + np.random.permutation(np.repeat(np.arange(E - 1), -(-T // (E - 1)))[:T])) % E
    while np.bincount(second, minlength=E).max() != T // E:
        load = np.bincount(second, minlength=E); hi, lo = int(load.argmax()), int(load.argmin())
        t = np.flatnonzero((second == hi) & (first != lo))[0]; second[t] = lo
    slot_token = np.empty(E * C, np.int64); pos = np.empty((2, T), np.int64); fill = np.zeros(E, np.int64)
    place = np.stack([np.random.permutation(C) for _ in range(E)])
    for r, deal in enumerate((first, second)):
        for t in np.random.permutation(T):
            e = deal[t]; j = e * C + place[e, fill[e]]; fill[e] += 1; slot_token[j] = t; pos[r, t] = j
    g = np.random.uniform(0.2, 0.8, T)
    return {
        "xT": (n((K, T)) * s).astype(np.float32),
        "w": (n((E, K, N)) / np.sqrt(K) / s[None]).astype(np.float32),
        "b": (0.3 * n((N, E))).astype(np.float32),
        "gate": np.stack([np.tile(g, (N, 1)), np.tile(1.0 - g, (N, 1))]).astype(np.float32),
        "offs": striped(slot_token),
        "pos1": striped(pos[0]),
        "pos2": striped(pos[1]),
    }


def reference(xT, w, b, gate, offs, pos1, pos2):
    idx = unstriped(offs)
    xq = mxq(f64(xT)[:, idx], 0, "e4m3")
    y = by_expert(mxq(f64(w), 1, "e4m3"), xq)
    y = gelu(y + np.repeat(f64(b), C, axis=1))
    return f64(gate[0]) * y[:, unstriped(pos1)] + f64(gate[1]) * y[:, unstriped(pos2)]

@@ -1,0 +1,225 @@
+from contextlib import ExitStack
+
+import concourse.mybir as mybir
+from concourse.masks import make_identity
+
+K, T, E, C, N = 512, 1024, 8, 256, 256
+FLOPS = 2 * K * N * E * C
+
+F32 = mybir.dt.float32
+BF16 = mybir.dt.bfloat16
+U32 = mybir.dt.uint32
+U16 = mybir.dt.uint16
+U8 = mybir.dt.uint8
+FP8X4 = mybir.dt.float8_e4m3fn_x4
+GELU = mybir.ActivationFunctionType.Gelu_apprx_tanh
+MULT = mybir.AluOpType.mult
+ADD = mybir.AluOpType.add
+
+P = 128
+PACK = 4
+XLOADS = (512, 256, 128, 128)
+XCHUNKS = (256, 256, 256, 128, 128)
+X_ON_SCALAR = (1,)
+PAIRS = E // 2
+GS = 2 * C
+H = N // P
+PIECES = ((0, 768), (768, 768), (1536, 512))
+STEPS = ((0, 0, 1024), (1, 0, 768), (1, 768, 256))
+PE_SUMS = ((0, 512), (512, 256))
+
+
+def interleave(copy, dst, src):
+    copy(
+        out=dst.rearrange("p (c i) j -> p c j i", i=4),
+        in_=src.rearrange("p j (c i) -> p c j i", i=4),
+    )
+
+
+def tile_routed_moe_kernel(tc, xT, w, b, gate, offs, pos1, pos2, out):
+    nc = tc.nc
+    with ExitStack() as ctx:
+        lists = ctx.enter_context(tc.tile_pool(name="lists", bufs=1))
+        keep = ctx.enter_context(tc.tile_pool(name="keep", bufs=1))
+        psum = ctx.enter_context(tc.psum_pool(name="psum", bufs=1))
+
+        xv = xT.rearrange("(p j) t -> p j t", j=PACK)
+        xstart = [sum(XCHUNKS[:c]) for c in range(len(XCHUNKS))]
+        xraw = {}
+        t0 = 0
+        for c, n in enumerate(XLOADS):
+            r = keep.tile([P, PACK, n], F32, name="xraw%d" % c)
+            nc.sync.dma_start(out=r[:], in_=xv[:, :, t0:t0 + n])
+            for k, s in enumerate(xstart):
+                if t0 <= s < t0 + n:
+                    xraw[k] = r[:, :, s - t0:s - t0 + XCHUNKS[k]]
+            t0 += n
+        offs_t = lists.tile([P, E * C // 16], U16, name="offs_t")
+        nc.sync.dma_start(offs_t[:], offs)
+        bt = keep.tile([P, H, E], F32, name="bt")
+        nc.sync.dma_start(out=bt[:].rearrange("p h e -> p (h e)"), in_=b.rearrange("(p h) e -> p (h e)", h=H))
+        wraw = []
+        for e in range(E):
+            r = keep.tile([P, PACK, N], F32, name="wraw%d" % e, tag="wraw%d" % e, align_bytes=64)
+            nc.sync.dma_start(out=r[:], in_=w[e].rearrange("(p j) n -> p j n", j=PACK))
+            wraw.append(r)
+        pos_t = []
+        for r, lst in enumerate((pos1, pos2)):
+            t = lists.tile([P, T // 16], U16, name="pos_t%d" % r)
+            nc.sync.dma_start(t[:], lst)
+            pos_t.append(t)
+        gate_t = {}
+        for h in range(H):
+            for r in range(2):
+                g = keep.tile([P, T], F32, name="gate_t%d_%d" % (r, h))
+                nc.sync.dma_start(out=g[:], in_=gate[r].rearrange("(p h) t -> p h t", h=H)[:, h, :])
+                gate_t[(r, h)] = g
+
+        warm = keep.tile([P, 1], F32, name="warm")
+        warm2 = keep.tile([P, 1], F32, name="warm2")
+        nc.vector.memset(warm[:], 0.0)
+        nc.scalar.activation(out=warm2[:], in_=warm[:], func=GELU)
+
+        xcodes = keep.tile([P, T], U32, name="xcodes", tag="xcodes", align_bytes=64)
+        xscales = keep.tile([P, T], U8, name="xscales", align_bytes=64)
+        nc.gpsimd.memset(xscales[:], 0)
+        ident = keep.tile([P, P], F32, name="ident")
+        make_identity(nc, ident[:])
+        xg = []
+
+        def xcopy(c):
+            g = keep.tile([P, XCHUNKS[c], PACK], BF16, name="xg%d" % c, align_bytes=64)
+            interleave(nc.scalar.copy if c in X_ON_SCALAR else nc.vector.tensor_copy, g[:], xraw[c])
+            xg.append(g)
+
+        def xquant(c):
+            nc.vector.quantize_mx(
+                out=xcodes[:, xstart[c]:xstart[c] + XCHUNKS[c]].bitcast(FP8X4),
+                scales=xscales[:, xstart[c]:xstart[c] + XCHUNKS[c]],
+                in_=xg[c][:].rearrange("p t j -> p (t j)"),
+            )
+
+        xcopy(0)
+        for c in range(1, len(XCHUNKS)):
+            xcopy(c)
+            xquant(c - 1)
+        xquant(len(XCHUNKS) - 1)
+
+        wg = [keep.tile([P, H, 4, P, PACK], BF16, name="wg%d" % f, align_bytes=64) for f in range(2)]
+
+        def winterleave(copy, e):
+            copy(
+                out=wg[e // 4][:, :, e % 4].rearrange("p h (c a) j -> p c j a h", a=2),
+                in_=wraw[e][:].rearrange("p j (c a h) -> p c j a h", a=2, h=H),
+            )
+
+        def winterleave_half(copy, e, h):
+            copy(
+                out=wg[e // 4][:, h, e % 4].rearrange("p (c a) j -> p c j a", a=2),
+                in_=wraw[e][:].rearrange("p j (c a h) -> p h c j a", a=2, h=H)[:, h],
+            )
+
+        for e in range(E - 1):
+            winterleave(nc.scalar.copy, e)
+        winterleave_half(nc.scalar.copy, E - 1, 1)
+
+        gc, gs = [], []
+
+        def gather_codes(i):
+            s0, n = PIECES[i]
+            c_ = keep.tile([P, n], U32, name="gc%d" % i, tag="wraw7" if i == 2 else "gc%d" % i, align_bytes=64)
+            nc.vector.tensor_copy(out=c_[:], in_=xcodes[:].indirect(offs_t[:, s0 // 16:(s0 + n) // 16]))
+            gc.append(c_)
+
+        def gather_scales(i):
+            s0, n = PIECES[i]
+            s_ = keep.tile([P, n], U8, name="gs%d" % i, align_bytes=64)
+            nc.vector.tensor_copy(out=s_[:], in_=xscales[:].indirect(offs_t[:, s0 // 16:(s0 + n) // 16]))
+            gs.append(s_)
+
+        for i in range(2):
+            gather_codes(i)
+            gather_scales(i)
+        gather_scales(2)
+
+        y = [keep.tile([P, E * C], F32, name="y%d" % h, tag="wraw6" if h == 0 else "y1", align_bytes=64) for h in range(H)]
+        wc, ws = {}, {}
+
+        banks = {}
+
+        def sums(e, h):
+            key, col = ((h, e // 2), e % 2) if e < 6 else ((e % 2, 3), h)
+            if key not in banks:
+                banks[key] = psum.tile([P, GS], F32, name="acc%d_%d" % key, tag="bank%d_%d" % key)
+            return banks[key][:, col * C:(col + 1) * C]
+
+        def products(i, h):
+            for u in range(2):
+                e = 2 * i + u
+                cols = slice((e % 4) * P, (e % 4 + 1) * P)
+                nc.tensor.matmul_mx(
+                    out=sums(e, h),
+                    lhsT=wc[(h, e // 4)][:, cols].bitcast(FP8X4),
+                    lhsT_scale=ws[(h, e // 4)][:, cols],
+                    rhs=gc[e // 3][:, (e % 3) * C:(e % 3 + 1) * C].bitcast(FP8X4),
+                    rhs_scale=gs[e // 3][:, (e % 3) * C:(e % 3 + 1) * C],
+                    start=True,
+                    stop=True,
+                )
+            for u in range(2):
+                e = 2 * i + u
+                nc.scalar.activation(
+                    out=y[h][:, e * C:(e + 1) * C],
+                    in_=sums(e, h),
+                    func=GELU,
+                    bias=bt[:, h, e:e + 1],
+                )
+
+        def wquant(h, f, c_):
+            s_ = keep.tile([P, 4 * P], U8, name="ws%d_%d" % (h, f), align_bytes=64)
+            nc.vector.quantize_mx(
+                out=c_.bitcast(FP8X4),
+                scales=s_[:],
+                in_=wg[f][:, h].rearrange("p v n j -> p (v n j)"),
+            )
+            wc[(h, f)] = c_
+            ws[(h, f)] = s_
+
+        wc0 = keep.tile([P, 8 * P], U32, name="wc0", align_bytes=64)
+        wquant(0, 0, wc0[:, 0:4 * P])
+        products(0, 0)
+        products(1, 0)
+        winterleave_half(nc.vector.tensor_copy, E - 1, 0)
+        wquant(0, 1, wc0[:, 4 * P:8 * P])
+        products(2, 0)
+        gather_codes(2)
+        products(3, 0)
+        wc1 = keep.tile([P, 8 * P], U32, name="wc1", tag="xcodes", align_bytes=64)
+        for f in range(2):
+            wquant(1, f, wc1[:, f * 4 * P:(f + 1) * 4 * P])
+        for i in range(PAIRS):
+            products(i, 1)
+
+        for h, t0, n in STEPS:
+            part = []
+            for r in range(2):
+                t = keep.tile([P, n], F32, name="part%d_%d_%d" % (r, h, t0), tag="part%d" % r, bufs=2)
+                nc.vector.tensor_tensor(
+                    out=t[:],
+                    in0=y[h][:].indirect(pos_t[r][:, t0 // 16:(t0 + n) // 16]),
+                    in1=gate_t[(r, h)][:, t0:t0 + n],
+                    op=MULT,
+                )
+                part.append(t)
+            o = keep.tile([P, n], F32, name="o%d_%d" % (h, t0))
+            v0 = 0
+            if h == 0:
+                for k, (a, m) in enumerate(PE_SUMS):
+                    total = psum.tile([P, m], F32, name="total%d" % k, tag="bank0_%d" % k)
+                    for r in range(2):
+                        nc.tensor.matmul(out=total[:], lhsT=ident[:], rhs=part[r][:, a:a + m], start=(r == 0), stop=(r == 1))
+                    nc.scalar.copy(out=o[:, a:a + m], in_=total[:])
+                    v0 = a + m
+            nc.vector.tensor_tensor(out=o[:, v0:], in0=part[0][:, v0:], in1=part[1][:, v0:], op=ADD)
+            queue = nc.scalar if h == 0 else nc.sync
+            queue.dma_start(out=out.rearrange("(p h) t -> p h t", h=H)[:, h, t0:t0 + n], in_=o[:])

@@ -107,21 +107,19 @@ def tile_routed_moe_kernel(tc, xT, w, b, gate, offs, pos1, pos2, out):
 
         wg = [keep.tile([P, H, 4, P, PACK], BF16, name="wg%d" % f, align_bytes=64) for f in range(2)]
 
-        def winterleave(copy, e):
-            copy(
-                out=wg[e // 4][:, :, e % 4].rearrange("p h (c a) j -> p c j a h", a=2),
-                in_=wraw[e][:].rearrange("p j (c a h) -> p c j a h", a=2, h=H),
-            )
-
         def winterleave_half(copy, e, h):
             copy(
                 out=wg[e // 4][:, h, e % 4].rearrange("p (c a) j -> p c j a", a=2),
                 in_=wraw[e][:].rearrange("p j (c a h) -> p h c j a", a=2, h=H)[:, h],
             )
 
-        for e in range(E - 1):
-            winterleave(nc.scalar.copy, e)
-        winterleave_half(nc.scalar.copy, E - 1, 1)
+        def gpsimd_copy(out, in_):
+            nc.gpsimd.tensor_scalar(out=out, in0=in_, scalar1=1.0, scalar2=0.0, op0=MULT, op1=ADD)
+
+        for e in range(E):
+            winterleave_half(nc.scalar.copy, e, 0)
+        for e in range(E):
+            winterleave_half(gpsimd_copy if e < 4 else nc.scalar.copy, e, 1)
 
         gc, gs = [], []
 
@@ -189,7 +187,6 @@ def tile_routed_moe_kernel(tc, xT, w, b, gate, offs, pos1, pos2, out):
         wquant(0, 0, wc0[:, 0:4 * P])
         products(0, 0)
         products(1, 0)
-        winterleave_half(nc.vector.tensor_copy, E - 1, 0)
         wquant(0, 1, wc0[:, 4 * P:8 * P])
         products(2, 0)
         gather_codes(2)

@@ -9,6 +9,7 @@ FLOPS = 2 * K * N * E * C
 F32 = mybir.dt.float32
 BF16 = mybir.dt.bfloat16
 U32 = mybir.dt.uint32
+I32 = mybir.dt.int32
 U16 = mybir.dt.uint16
 U8 = mybir.dt.uint8
 FP8X4 = mybir.dt.float8_e4m3fn_x4
@@ -24,7 +25,8 @@ X_ON_SCALAR = (1,)
 PAIRS = E // 2
 GS = 2 * C
 H = N // P
-PIECES = ((0, 768), (768, 768), (1536, 512))
+PIECES = ((0, 1536), (1536, 512))
+WINDOW = 2 * T
 STEPS = ((0, 0, 1024), (1, 0, 768), (1, 768, 256))
 PE_SUMS = ((0, 512), (512, 256))
 
@@ -80,8 +82,9 @@ def tile_routed_moe_kernel(tc, xT, w, b, gate, offs, pos1, pos2, out):
         nc.vector.memset(warm[:], 0.0)
         nc.scalar.activation(out=warm2[:], in_=warm[:], func=GELU)
 
-        xcodes = keep.tile([P, T], U32, name="xcodes", tag="xcodes", align_bytes=64)
-        xscales = keep.tile([P, T], U8, name="xscales", align_bytes=64)
+        xcodes = keep.tile([P, WINDOW], I32, name="xcodes", tag="xcodes", align_bytes=64)
+        xscales = keep.tile([P, WINDOW], U8, name="xscales", align_bytes=64)
+        nc.vector.memset(xcodes[:, T:WINDOW], 0)
         nc.gpsimd.memset(xscales[:], 0)
         ident = keep.tile([P, P], F32, name="ident")
         make_identity(nc, ident[:])
@@ -125,8 +128,8 @@ def tile_routed_moe_kernel(tc, xT, w, b, gate, offs, pos1, pos2, out):
 
         def gather_codes(i):
             s0, n = PIECES[i]
-            c_ = keep.tile([P, n], U32, name="gc%d" % i, tag="wraw7" if i == 2 else "gc%d" % i, align_bytes=64)
-            nc.vector.tensor_copy(out=c_[:], in_=xcodes[:].indirect(offs_t[:, s0 // 16:(s0 + n) // 16]))
+            c_ = keep.tile([P, n], U32, name="gc%d" % i, tag="wraw7" if i == 1 else "gc%d" % i, align_bytes=64)
+            nc.vector.tensor_copy(out=c_[:], in_=xcodes[:].bitcast(U32).indirect(offs_t[:, s0 // 16:(s0 + n) // 16]))
             gc.append(c_)
 
         def gather_scales(i):
@@ -135,10 +138,9 @@ def tile_routed_moe_kernel(tc, xT, w, b, gate, offs, pos1, pos2, out):
             nc.vector.tensor_copy(out=s_[:], in_=xscales[:].indirect(offs_t[:, s0 // 16:(s0 + n) // 16]))
             gs.append(s_)
 
-        for i in range(2):
-            gather_codes(i)
-            gather_scales(i)
-        gather_scales(2)
+        gather_codes(0)
+        gather_scales(0)
+        gather_scales(1)
 
         y = [keep.tile([P, E * C], F32, name="y%d" % h, tag="wraw6" if h == 0 else "y1", align_bytes=64) for h in range(H)]
         wc, ws = {}, {}
@@ -159,8 +161,8 @@ def tile_routed_moe_kernel(tc, xT, w, b, gate, offs, pos1, pos2, out):
                     out=sums(e, h),
                     lhsT=wc[(h, e // 4)][:, cols].bitcast(FP8X4),
                     lhsT_scale=ws[(h, e // 4)][:, cols],
-                    rhs=gc[e // 3][:, (e % 3) * C:(e % 3 + 1) * C].bitcast(FP8X4),
-                    rhs_scale=gs[e // 3][:, (e % 3) * C:(e % 3 + 1) * C],
+                    rhs=gc[e // 6][:, (e % 6) * C:(e % 6 + 1) * C].bitcast(FP8X4),
+                    rhs_scale=gs[e // 6][:, (e % 6) * C:(e % 6 + 1) * C],
                     start=True,
                     stop=True,
                 )
@@ -189,7 +191,7 @@ def tile_routed_moe_kernel(tc, xT, w, b, gate, offs, pos1, pos2, out):
         products(1, 0)
         wquant(0, 1, wc0[:, 4 * P:8 * P])
         products(2, 0)
-        gather_codes(2)
+        gather_codes(1)
         products(3, 0)
         wc1 = keep.tile([P, 8 * P], U32, name="wc1", tag="xcodes", align_bytes=64)
         for f in range(2):

@@ -59,7 +59,7 @@ def tile_routed_moe_kernel(tc, xT, w, b, gate, offs, pos1, pos2, out):
         offs_t = lists.tile([P, E * C // 16], U16, name="offs_t")
         nc.sync.dma_start(offs_t[:], offs)
         bt = keep.tile([P, H, E], F32, name="bt")
-        nc.sync.dma_start(out=bt[:].rearrange("p h e -> p (h e)"), in_=b.rearrange("(p h) e -> p (h e)", h=H))
+        nc.sync.dma_start(out=bt[:], in_=b.rearrange("(h p) e -> p h e", h=H))
         wraw = []
         for e in range(E):
             r = keep.tile([P, PACK, N], F32, name="wraw%d" % e, tag="wraw%d" % e, align_bytes=64)
@@ -74,7 +74,7 @@ def tile_routed_moe_kernel(tc, xT, w, b, gate, offs, pos1, pos2, out):
         for h in range(H):
             for r in range(2):
                 g = keep.tile([P, T], F32, name="gate_t%d_%d" % (r, h))
-                nc.sync.dma_start(out=g[:], in_=gate[r].rearrange("(p h) t -> p h t", h=H)[:, h, :])
+                nc.sync.dma_start(out=g[:], in_=gate[r][h * P:(h + 1) * P, :])
                 gate_t[(r, h)] = g
 
         warm = keep.tile([P, 1], F32, name="warm")
@@ -111,18 +111,22 @@ def tile_routed_moe_kernel(tc, xT, w, b, gate, offs, pos1, pos2, out):
         wg = [keep.tile([P, H, 4, P, PACK], BF16, name="wg%d" % f, align_bytes=64) for f in range(2)]
 
         def winterleave_half(copy, e, h):
-            copy(
-                out=wg[e // 4][:, h, e % 4].rearrange("p (c a) j -> p c j a", a=2),
-                in_=wraw[e][:].rearrange("p j (c a h) -> p h c j a", a=2, h=H)[:, h],
-            )
+            interleave(copy, wg[e // 4][:, h, e % 4], wraw[e][:, :, h * P:(h + 1) * P])
 
-        def gpsimd_copy(out, in_):
-            nc.gpsimd.tensor_scalar(out=out, in0=in_, scalar1=1.0, scalar2=0.0, op0=MULT, op1=ADD)
+        def winterleave_half_gpsimd(e, h):
+            nc.gpsimd.tensor_scalar(
+                out=wg[e // 4][:, h, e % 4],
+                in0=wraw[e][:, :, h * P:(h + 1) * P].rearrange("p j n -> p n j"),
+                scalar1=1.0, scalar2=0.0, op0=MULT, op1=ADD,
+            )
 
         for e in range(E):
             winterleave_half(nc.scalar.copy, e, 0)
         for e in range(E):
-            winterleave_half(gpsimd_copy if e < 4 else nc.scalar.copy, e, 1)
+            if e < 4:
+                winterleave_half_gpsimd(e, 1)
+            else:
+                winterleave_half(nc.scalar.copy, e, 1)
 
         gc, gs = [], []
 
@@ -221,4 +225,4 @@ def tile_routed_moe_kernel(tc, xT, w, b, gate, offs, pos1, pos2, out):
                     v0 = a + m
             nc.vector.tensor_tensor(out=o[:, v0:], in0=part[0][:, v0:], in1=part[1][:, v0:], op=ADD)
             queue = nc.scalar if h == 0 else nc.sync
-            queue.dma_start(out=out.rearrange("(p h) t -> p h t", h=H)[:, h, t0:t0 + n], in_=o[:])
+            queue.dma_start(out=out[h * P:(h + 1) * P, t0:t0 + n], in_=o[:])

@@ -123,7 +123,7 @@ def tile_routed_moe_kernel(tc, xT, w, b, gate, offs, pos1, pos2, out):
         for e in range(E):
             winterleave_half(nc.scalar.copy, e, 0)
         for e in range(E):
-            if e < 4:
+            if e < 5:
                 winterleave_half_gpsimd(e, 1)
             else:
                 winterleave_half(nc.scalar.copy, e, 1)

@@ -26,6 +26,7 @@ PAIRS = E // 2
 GS = 2 * C
 H = N // P
 PIECES = ((0, 1536), (1536, 512))
+CODE_CUTS = ((1536,), (256, 256))
 WINDOW = 2 * T
 STEPS = ((0, 0, 1024), (1, 0, 768), (1, 768, 256))
 PE_SUMS = ((0, 512), (512, 256))
@@ -133,12 +134,15 @@ def tile_routed_moe_kernel(tc, xT, w, b, gate, offs, pos1, pos2, out):
         def gather_codes(i):
             s0, n = PIECES[i]
             c_ = keep.tile([P, n], U32, name="gc%d" % i, tag="wraw7" if i == 1 else "gc%d" % i, align_bytes=64)
-            nc.vector.tensor_copy(out=c_[:], in_=xcodes[:].bitcast(U32).indirect(offs_t[:, s0 // 16:(s0 + n) // 16]))
+            a = 0
+            for m in CODE_CUTS[i]:
+                nc.vector.tensor_copy(out=c_[:, a:a + m], in_=xcodes[:].bitcast(U32).indirect(offs_t[:, (s0 + a) // 16:(s0 + a + m) // 16]))
+                a += m
             gc.append(c_)
 
         def gather_scales(i):
             s0, n = PIECES[i]
-            s_ = keep.tile([P, n], U8, name="gs%d" % i, align_bytes=64)
+            s_ = keep.tile([P, n], U8, name="gs%d" % i, tag="wraw4" if i == 1 else "gs%d" % i, align_bytes=64)
             nc.vector.tensor_copy(out=s_[:], in_=xscales[:].indirect(offs_t[:, s0 // 16:(s0 + n) // 16]))
             gs.append(s_)
 
@@ -197,10 +201,11 @@ def tile_routed_moe_kernel(tc, xT, w, b, gate, offs, pos1, pos2, out):
         products(2, 0)
         gather_codes(1)
         products(3, 0)
-        wc1 = keep.tile([P, 8 * P], U32, name="wc1", tag="xcodes", align_bytes=64)
-        for f in range(2):
-            wquant(1, f, wc1[:, f * 4 * P:(f + 1) * 4 * P])
-        for i in range(PAIRS):
+        wc1b = keep.tile([P, 4 * P], U32, name="wc1b", align_bytes=64)
+        wquant(1, 1, wc1b[:])
+        wc1a = keep.tile([P, 4 * P], U32, name="wc1a", tag="xcodes", align_bytes=64)
+        wquant(1, 0, wc1a[:])
+        for i in (2, 3, 0, 1):
             products(i, 1)
 
         for h, t0, n in STEPS:

@@ -19,9 +19,9 @@ ADD = mybir.AluOpType.add
 
 P = 128
 PACK = 4
-XLOADS = (512, 256, 128, 128)
+XLOADS = (512, 256, 256)
 XCHUNKS = (256, 256, 256, 128, 128)
-X_ON_SCALAR = (1,)
+X_ON_SCALAR = (1, 3)
 PAIRS = E // 2
 GS = 2 * C
 H = N // P

@@ -28,7 +28,7 @@ H = N // P
 PIECES = ((0, 1536), (1536, 512))
 CODE_CUTS = ((1536,), (256, 256))
 WINDOW = 2 * T
-STEPS = ((0, 0, 1024), (1, 0, 768), (1, 768, 256))
+STEPS = ((0, 0, (1024,)), (1, 0, (768,)), (1, 768, (192, 256)))
 PE_SUMS = ((0, 512), (512, 256))
 
 
@@ -124,7 +124,7 @@ def tile_routed_moe_kernel(tc, xT, w, b, gate, offs, pos1, pos2, out):
         for e in range(E):
             winterleave_half(nc.scalar.copy, e, 0)
         for e in range(E):
-            if e < 5:
+            if e < 2:
                 winterleave_half_gpsimd(e, 1)
             else:
                 winterleave_half(nc.scalar.copy, e, 1)
@@ -208,16 +208,20 @@ def tile_routed_moe_kernel(tc, xT, w, b, gate, offs, pos1, pos2, out):
         for i in (2, 3, 0, 1):
             products(i, 1)
 
-        for h, t0, n in STEPS:
+        for h, t0, ends in STEPS:
+            n = ends[-1]
             part = []
             for r in range(2):
                 t = keep.tile([P, n], F32, name="part%d_%d_%d" % (r, h, t0), tag="part%d" % r, bufs=2)
-                nc.vector.tensor_tensor(
-                    out=t[:],
-                    in0=y[h][:].indirect(pos_t[r][:, t0 // 16:(t0 + n) // 16]),
-                    in1=gate_t[(r, h)][:, t0:t0 + n],
-                    op=MULT,
-                )
+                a = 0
+                for b_ in (ends if r == 1 else (n,)):
+                    nc.vector.tensor_tensor(
+                        out=t[:, a:b_],
+                        in0=y[h][:].indirect(pos_t[r][:, (t0 + a) // 16:(t0 + b_) // 16]),
+                        in1=gate_t[(r, h)][:, t0 + a:t0 + b_],
+                        op=MULT,
+                    )
+                    a = b_
                 part.append(t)
             o = keep.tile([P, n], F32, name="o%d_%d" % (h, t0))
             v0 = 0
@@ -228,6 +232,8 @@ def tile_routed_moe_kernel(tc, xT, w, b, gate, offs, pos1, pos2, out):
                         nc.tensor.matmul(out=total[:], lhsT=ident[:], rhs=part[r][:, a:a + m], start=(r == 0), stop=(r == 1))
                     nc.scalar.copy(out=o[:, a:a + m], in_=total[:])
                     v0 = a + m
-            nc.vector.tensor_tensor(out=o[:, v0:], in0=part[0][:, v0:], in1=part[1][:, v0:], op=ADD)
+            for b_ in ends:
+                nc.vector.tensor_tensor(out=o[:, v0:b_], in0=part[0][:, v0:b_], in1=part[1][:, v0:b_], op=ADD)
+                v0 = b_
             queue = nc.scalar if h == 0 else nc.sync
             queue.dma_start(out=out[h * P:(h + 1) * P, t0:t0 + n], in_=o[:])

@@ -20,16 +20,15 @@ ADD = mybir.AluOpType.add
 P = 128
 PACK = 4
 XLOADS = (512, 256, 256)
-XCHUNKS = (256, 256, 256, 128, 128)
-X_ON_SCALAR = (1, 3)
+XCOPIES = ((0, 256), (256, 256), (512, 256), (768, 128), (896, 128))
 PAIRS = E // 2
 GS = 2 * C
 H = N // P
 PIECES = ((0, 1536), (1536, 512))
 CODE_CUTS = ((1536,), (256, 256))
 WINDOW = 2 * T
-STEPS = ((0, 0, (1024,)), (1, 0, (768,)), (1, 768, (192, 256)))
-PE_SUMS = ((0, 512), (512, 256))
+PE_COLS = 768
+LAST = 256
 
 
 def interleave(copy, dst, src):
@@ -47,15 +46,14 @@ def tile_routed_moe_kernel(tc, xT, w, b, gate, offs, pos1, pos2, out):
         psum = ctx.enter_context(tc.psum_pool(name="psum", bufs=1))
 
         xv = xT.rearrange("(p j) t -> p j t", j=PACK)
-        xstart = [sum(XCHUNKS[:c]) for c in range(len(XCHUNKS))]
         xraw = {}
         t0 = 0
         for c, n in enumerate(XLOADS):
             r = keep.tile([P, PACK, n], F32, name="xraw%d" % c)
             nc.sync.dma_start(out=r[:], in_=xv[:, :, t0:t0 + n])
-            for k, s in enumerate(xstart):
-                if t0 <= s < t0 + n:
-                    xraw[k] = r[:, :, s - t0:s - t0 + XCHUNKS[k]]
+            for s0, m in XCOPIES:
+                if t0 <= s0 < t0 + n:
+                    xraw[s0] = r[:, :, s0 - t0:s0 - t0 + m]
             t0 += n
         offs_t = lists.tile([P, E * C // 16], U16, name="offs_t")
         nc.sync.dma_start(offs_t[:], offs)
@@ -83,40 +81,45 @@ def tile_routed_moe_kernel(tc, xT, w, b, gate, offs, pos1, pos2, out):
         nc.vector.memset(warm[:], 0.0)
         nc.scalar.activation(out=warm2[:], in_=warm[:], func=GELU)
 
-        xcodes = keep.tile([P, WINDOW], I32, name="xcodes", tag="xcodes", align_bytes=64)
+        xcodes = keep.tile([P, WINDOW], I32, name="xcodes", align_bytes=64)
         xscales = keep.tile([P, WINDOW], U8, name="xscales", align_bytes=64)
         nc.vector.memset(xcodes[:, T:WINDOW], 0)
         nc.gpsimd.memset(xscales[:], 0)
         ident = keep.tile([P, P], F32, name="ident")
         make_identity(nc, ident[:])
-        xg = []
+        xg = {}
 
-        def xcopy(c):
-            g = keep.tile([P, XCHUNKS[c], PACK], BF16, name="xg%d" % c, align_bytes=64)
-            interleave(nc.scalar.copy if c in X_ON_SCALAR else nc.vector.tensor_copy, g[:], xraw[c])
-            xg.append(g)
+        def xcopy(copy, s0, n, q0, m):
+            if q0 not in xg:
+                g = keep.tile([P, m, PACK], BF16, name="xg%d" % q0, align_bytes=64)
+                xg[q0] = g
+            interleave(copy, xg[q0][:, s0 - q0:s0 - q0 + n], xraw[s0])
 
-        def xquant(c):
+        def xquant(q0, m):
             nc.vector.quantize_mx(
-                out=xcodes[:, xstart[c]:xstart[c] + XCHUNKS[c]].bitcast(FP8X4),
-                scales=xscales[:, xstart[c]:xstart[c] + XCHUNKS[c]],
-                in_=xg[c][:].rearrange("p t j -> p (t j)"),
+                out=xcodes[:, q0:q0 + m].bitcast(FP8X4),
+                scales=xscales[:, q0:q0 + m],
+                in_=xg[q0][:].rearrange("p t j -> p (t j)"),
             )
 
-        xcopy(0)
-        for c in range(1, len(XCHUNKS)):
-            xcopy(c)
-            xquant(c - 1)
-        xquant(len(XCHUNKS) - 1)
+        xcopy(nc.vector.tensor_copy, 0, 256, 0, 256)
+        xcopy(nc.scalar.copy, 256, 256, 256, 256)
+        xquant(0, 256)
+        xcopy(nc.vector.tensor_copy, 512, 256, 512, 256)
+        xquant(256, 256)
+        xcopy(nc.vector.tensor_copy, 768, 128, 768, 256)
+        xcopy(nc.scalar.copy, 896, 128, 768, 256)
+        xquant(512, 256)
+        xquant(768, 256)
 
-        wg = [keep.tile([P, H, 4, P, PACK], BF16, name="wg%d" % f, align_bytes=64) for f in range(2)]
+        wg = [keep.tile([P, E, P, PACK], BF16, name="wg%d" % h, align_bytes=64) for h in range(H)]
 
         def winterleave_half(copy, e, h):
-            interleave(copy, wg[e // 4][:, h, e % 4], wraw[e][:, :, h * P:(h + 1) * P])
+            interleave(copy, wg[h][:, e], wraw[e][:, :, h * P:(h + 1) * P])
 
         def winterleave_half_gpsimd(e, h):
             nc.gpsimd.tensor_scalar(
-                out=wg[e // 4][:, h, e % 4],
+                out=wg[h][:, e],
                 in0=wraw[e][:, :, h * P:(h + 1) * P].rearrange("p j n -> p n j"),
                 scalar1=1.0, scalar2=0.0, op0=MULT, op1=ADD,
             )
@@ -164,11 +167,10 @@ def tile_routed_moe_kernel(tc, xT, w, b, gate, offs, pos1, pos2, out):
         def products(i, h):
             for u in range(2):
                 e = 2 * i + u
-                cols = slice((e % 4) * P, (e % 4 + 1) * P)
                 nc.tensor.matmul_mx(
                     out=sums(e, h),
-                    lhsT=wc[(h, e // 4)][:, cols].bitcast(FP8X4),
-                    lhsT_scale=ws[(h, e // 4)][:, cols],
+                    lhsT=wc[(h, e)].bitcast(FP8X4),
+                    lhsT_scale=ws[(h, e)],
                     rhs=gc[e // 6][:, (e % 6) * C:(e % 6 + 1) * C].bitcast(FP8X4),
                     rhs_scale=gs[e // 6][:, (e % 6) * C:(e % 6 + 1) * C],
                     start=True,
@@ -183,57 +185,64 @@ def tile_routed_moe_kernel(tc, xT, w, b, gate, offs, pos1, pos2, out):
                     bias=bt[:, h, e:e + 1],
                 )
 
-        def wquant(h, f, c_):
-            s_ = keep.tile([P, 4 * P], U8, name="ws%d_%d" % (h, f), align_bytes=64)
+        def wquant(h, e0, n):
+            c_ = keep.tile([P, n * P], U32, name="wc%d_%d" % (h, e0), align_bytes=64)
+            s_ = keep.tile([P, n * P], U8, name="ws%d_%d" % (h, e0), align_bytes=64)
             nc.vector.quantize_mx(
-                out=c_.bitcast(FP8X4),
+                out=c_[:].bitcast(FP8X4),
                 scales=s_[:],
-                in_=wg[f][:, h].rearrange("p v n j -> p (v n j)"),
+                in_=wg[h][:, e0:e0 + n].rearrange("p v n j -> p (v n j)"),
             )
-            wc[(h, f)] = c_
-            ws[(h, f)] = s_
+            for v in range(n):
+                wc[(h, e0 + v)] = c_[:, v * P:(v + 1) * P]
+                ws[(h, e0 + v)] = s_[:, v * P:(v + 1) * P]
 
-        wc0 = keep.tile([P, 8 * P], U32, name="wc0", align_bytes=64)
-        wquant(0, 0, wc0[:, 0:4 * P])
+        wquant(0, 0, 4)
         products(0, 0)
         products(1, 0)
-        wquant(0, 1, wc0[:, 4 * P:8 * P])
+        wquant(0, 4, 4)
         products(2, 0)
         gather_codes(1)
         products(3, 0)
-        wc1b = keep.tile([P, 4 * P], U32, name="wc1b", align_bytes=64)
-        wquant(1, 1, wc1b[:])
-        wc1a = keep.tile([P, 4 * P], U32, name="wc1a", tag="xcodes", align_bytes=64)
-        wquant(1, 0, wc1a[:])
-        for i in (2, 3, 0, 1):
+        wquant(1, 0, 8)
+        for i in range(PAIRS):
             products(i, 1)
 
-        for h, t0, ends in STEPS:
-            n = ends[-1]
-            part = []
+        def gathered_product(r, h, t0, n, name, tag):
+            t = keep.tile([P, n], F32, name=name, tag=tag)
+            nc.vector.tensor_tensor(
+                out=t[:],
+                in0=y[h][:].indirect(pos_t[r][:, t0 // 16:(t0 + n) // 16]),
+                in1=gate_t[(r, h)][:, t0:t0 + n],
+                op=MULT,
+            )
+            return t
+
+        def store(queue, h, t0, n, tile_):
+            queue.dma_start(out=out[h * P:(h + 1) * P, t0:t0 + n], in_=tile_[:])
+
+        part = [gathered_product(r, 0, 0, T, "part%d_0" % r, "part%d_0" % r) for r in range(2)]
+        first = gathered_product(0, 1, 0, T, "part0_1", "part0_1")
+        second = gathered_product(1, 1, 0, T - LAST, "part1_1", "part1_1")
+
+        o = keep.tile([P, PE_COLS], F32, name="o_pe")
+        for k, a in enumerate(range(0, PE_COLS, 512)):
+            b_ = min(a + 512, PE_COLS)
+            total = psum.tile([P, b_ - a], F32, name="total%d" % k, tag="bank0_%d" % k)
             for r in range(2):
-                t = keep.tile([P, n], F32, name="part%d_%d_%d" % (r, h, t0), tag="part%d" % r, bufs=2)
-                a = 0
-                for b_ in (ends if r == 1 else (n,)):
-                    nc.vector.tensor_tensor(
-                        out=t[:, a:b_],
-                        in0=y[h][:].indirect(pos_t[r][:, (t0 + a) // 16:(t0 + b_) // 16]),
-                        in1=gate_t[(r, h)][:, t0 + a:t0 + b_],
-                        op=MULT,
-                    )
-                    a = b_
-                part.append(t)
-            o = keep.tile([P, n], F32, name="o%d_%d" % (h, t0))
-            v0 = 0
-            if h == 0:
-                for k, (a, m) in enumerate(PE_SUMS):
-                    total = psum.tile([P, m], F32, name="total%d" % k, tag="bank0_%d" % k)
-                    for r in range(2):
-                        nc.tensor.matmul(out=total[:], lhsT=ident[:], rhs=part[r][:, a:a + m], start=(r == 0), stop=(r == 1))
-                    nc.scalar.copy(out=o[:, a:a + m], in_=total[:])
-                    v0 = a + m
-            for b_ in ends:
-                nc.vector.tensor_tensor(out=o[:, v0:b_], in0=part[0][:, v0:b_], in1=part[1][:, v0:b_], op=ADD)
-                v0 = b_
-            queue = nc.scalar if h == 0 else nc.sync
-            queue.dma_start(out=out[h * P:(h + 1) * P, t0:t0 + n], in_=o[:])
+                nc.tensor.matmul(out=total[:], lhsT=ident[:], rhs=part[r][:, a:b_], start=(r == 0), stop=(r == 1))
+            nc.scalar.copy(out=o[:, a:b_], in_=total[:])
+        store(nc.scalar, 0, 0, PE_COLS, o)
+
+        o = keep.tile([P, T - PE_COLS], F32, name="o_rest", tag="gate_t0_1")
+        nc.vector.tensor_tensor(out=o[:], in0=part[0][:, PE_COLS:], in1=part[1][:, PE_COLS:], op=ADD)
+        store(nc.sync, 0, PE_COLS, T - PE_COLS, o)
+
+        o = keep.tile([P, T - LAST], F32, name="o_main")
+        nc.vector.tensor_tensor(out=o[:], in0=first[:, 0:T - LAST], in1=second[:], op=ADD)
+        store(nc.sync, 1, 0, T - LAST, o)
+
+        second = gathered_product(1, 1, T - LAST, LAST, "part1_last", "part1_0")
+        o = keep.tile([P, LAST], F32, name="o_last")
+        nc.vector.tensor_tensor(out=o[:], in0=first[:, T - LAST:], in1=second[:], op=ADD)
+        store(nc.sync, 1, T - LAST, LAST, o)

@@ -27,7 +27,7 @@ H = N // P
 PIECES = ((0, 1536), (1536, 512))
 CODE_CUTS = ((1536,), (256, 256))
 WINDOW = 2 * T
-PE_COLS = 768
+PE_COLS = 816
 LAST = 256
 
 
@@ -57,24 +57,30 @@ def tile_routed_moe_kernel(tc, xT, w, b, gate, offs, pos1, pos2, out):
             t0 += n
         offs_t = lists.tile([P, E * C // 16], U16, name="offs_t")
         nc.sync.dma_start(offs_t[:], offs)
-        bt = keep.tile([P, H, E], F32, name="bt")
-        nc.sync.dma_start(out=bt[:], in_=b.rearrange("(h p) e -> p h e", h=H))
         wraw = []
         for e in range(E):
             r = keep.tile([P, PACK, N], F32, name="wraw%d" % e, tag="wraw%d" % e, align_bytes=64)
-            nc.sync.dma_start(out=r[:], in_=w[e].rearrange("(p j) n -> p j n", j=PACK))
+            we = w[e].rearrange("(p j) n -> p j n", j=PACK)
+            for n0 in range(0, N, N if e < E - 1 else P):
+                n1 = n0 + (N if e < E - 1 else P)
+                nc.sync.dma_start(out=r[:, :, n0:n1], in_=we[:, :, n0:n1])
             wraw.append(r)
+        bt = keep.tile([P, H, E], F32, name="bt")
+        nc.sync.dma_start(out=bt[:], in_=b.rearrange("(h p) e -> p h e", h=H))
         pos_t = []
         for r, lst in enumerate((pos1, pos2)):
             t = lists.tile([P, T // 16], U16, name="pos_t%d" % r)
             nc.sync.dma_start(t[:], lst)
             pos_t.append(t)
         gate_t = {}
-        for h in range(H):
-            for r in range(2):
-                g = keep.tile([P, T], F32, name="gate_t%d_%d" % (r, h))
-                nc.sync.dma_start(out=g[:], in_=gate[r][h * P:(h + 1) * P, :])
-                gate_t[(r, h)] = g
+        g = keep.tile([P, 2, T], F32, name="gate_t_0")
+        nc.sync.dma_start(out=g[:], in_=gate[:, 0:P, :].rearrange("r p t -> p r t"))
+        for r in range(2):
+            gate_t[(r, 0)] = g[:, r, :]
+        for r in range(2):
+            g = keep.tile([P, T], F32, name="gate_t%d_1" % r)
+            nc.sync.dma_start(out=g[:], in_=gate[r][P:2 * P, :])
+            gate_t[(r, 1)] = g[:]
 
         warm = keep.tile([P, 1], F32, name="warm")
         warm2 = keep.tile([P, 1], F32, name="warm2")
@@ -117,20 +123,10 @@ def tile_routed_moe_kernel(tc, xT, w, b, gate, offs, pos1, pos2, out):
         def winterleave_half(copy, e, h):
             interleave(copy, wg[h][:, e], wraw[e][:, :, h * P:(h + 1) * P])
 
-        def winterleave_half_gpsimd(e, h):
-            nc.gpsimd.tensor_scalar(
-                out=wg[h][:, e],
-                in0=wraw[e][:, :, h * P:(h + 1) * P].rearrange("p j n -> p n j"),
-                scalar1=1.0, scalar2=0.0, op0=MULT, op1=ADD,
-            )
-
         for e in range(E):
             winterleave_half(nc.scalar.copy, e, 0)
         for e in range(E):
-            if e < 2:
-                winterleave_half_gpsimd(e, 1)
-            else:
-                winterleave_half(nc.scalar.copy, e, 1)
+            winterleave_half(nc.scalar.copy, e, 1)
 
         gc, gs = [], []
 

@@ -19,8 +19,8 @@ ADD = mybir.AluOpType.add
 
 P = 128
 PACK = 4
-XLOADS = (512, 256, 256)
-XCOPIES = ((0, 256), (256, 256), (512, 256), (768, 128), (896, 128))
+XLOADS = (512, 384, 128)
+XCOPIES = ((0, 256), (256, 256), (512, 256), (768, 128), (896, 64), (960, 64))
 PAIRS = E // 2
 GS = 2 * C
 H = N // P
@@ -113,10 +113,12 @@ def tile_routed_moe_kernel(tc, xT, w, b, gate, offs, pos1, pos2, out):
         xquant(0, 256)
         xcopy(nc.vector.tensor_copy, 512, 256, 512, 256)
         xquant(256, 256)
-        xcopy(nc.vector.tensor_copy, 768, 128, 768, 256)
-        xcopy(nc.scalar.copy, 896, 128, 768, 256)
+        xcopy(nc.scalar.copy, 768, 128, 768, 128)
         xquant(512, 256)
-        xquant(768, 256)
+        xcopy(nc.vector.tensor_copy, 896, 64, 896, 128)
+        xcopy(nc.scalar.copy, 960, 64, 896, 128)
+        xquant(768, 128)
+        xquant(896, 128)
 
         wg = [keep.tile([P, E, P, PACK], BF16, name="wg%d" % h, align_bytes=64) for h in range(H)]
 

@@ -25,7 +25,7 @@ PAIRS = E // 2
 GS = 2 * C
 H = N // P
 PIECES = ((0, 1536), (1536, 512))
-CODE_CUTS = ((1536,), (256, 256))
+CODE_CUTS = ((1536,), (384, 128))
 WINDOW = 2 * T
 PE_COLS = 816
 LAST = 256
@@ -137,7 +137,8 @@ def tile_routed_moe_kernel(tc, xT, w, b, gate, offs, pos1, pos2, out):
             c_ = keep.tile([P, n], U32, name="gc%d" % i, tag="wraw7" if i == 1 else "gc%d" % i, align_bytes=64)
             a = 0
             for m in CODE_CUTS[i]:
-                nc.vector.tensor_copy(out=c_[:, a:a + m], in_=xcodes[:].bitcast(U32).indirect(offs_t[:, (s0 + a) // 16:(s0 + a + m) // 16]))
+                window = xcodes[:] if m > C else xcodes[:, 0:T]
+                nc.vector.tensor_copy(out=c_[:, a:a + m], in_=window.bitcast(U32).indirect(offs_t[:, (s0 + a) // 16:(s0 + a + m) // 16]))
                 a += m
             gc.append(c_)
 
@@ -163,22 +164,25 @@ def tile_routed_moe_kernel(tc, xT, w, b, gate, offs, pos1, pos2, out):
             return banks[key][:, col * C:(col + 1) * C]
 
         def products(i, h):
-            for u in range(2):
-                e = 2 * i + u
+            cuts = []
+            for e in (2 * i, 2 * i + 1):
+                n = C // 2 if (e, h) == (E - 1, 0) else C
+                cuts += [(e, c0, n) for c0 in range(0, C, n)]
+            for e, c0, n in cuts:
+                s0 = (e % 6) * C + c0
                 nc.tensor.matmul_mx(
-                    out=sums(e, h),
+                    out=sums(e, h)[:, c0:c0 + n],
                     lhsT=wc[(h, e)].bitcast(FP8X4),
                     lhsT_scale=ws[(h, e)],
-                    rhs=gc[e // 6][:, (e % 6) * C:(e % 6 + 1) * C].bitcast(FP8X4),
-                    rhs_scale=gs[e // 6][:, (e % 6) * C:(e % 6 + 1) * C],
+                    rhs=gc[e // 6][:, s0:s0 + n].bitcast(FP8X4),
+                    rhs_scale=gs[e // 6][:, s0:s0 + n],
                     start=True,
                     stop=True,
                 )
-            for u in range(2):
-                e = 2 * i + u
+            for e, c0, n in cuts:
                 nc.scalar.activation(
-                    out=y[h][:, e * C:(e + 1) * C],
-                    in_=sums(e, h),
+                    out=y[h][:, e * C + c0:e * C + c0 + n],
+                    in_=sums(e, h)[:, c0:c0 + n],
                     func=GELU,
                     bias=bt[:, h, e:e + 1],
                 )

from contextlib import ExitStack

import concourse.mybir as mybir
from concourse.masks import make_identity

K, T, E, C, N = 512, 1024, 8, 256, 256
FLOPS = 2 * K * N * E * C

F32 = mybir.dt.float32
BF16 = mybir.dt.bfloat16
U32 = mybir.dt.uint32
I32 = mybir.dt.int32
U16 = mybir.dt.uint16
U8 = mybir.dt.uint8
FP8X4 = mybir.dt.float8_e4m3fn_x4
GELU = mybir.ActivationFunctionType.Gelu_apprx_tanh
MULT = mybir.AluOpType.mult
ADD = mybir.AluOpType.add

P = 128
PACK = 4
XLOADS = (512, 384, 128)
XCOPIES = ((0, 256), (256, 256), (512, 256), (768, 128), (896, 64), (960, 64))
PAIRS = E // 2
GS = 2 * C
H = N // P
PIECES = ((0, 1536), (1536, 512))
CODE_CUTS = ((1536,), (384, 128))
WINDOW = 2 * T
PE_COLS = 816
LAST = 256


def interleave(copy, dst, src):
    copy(
        out=dst.rearrange("p (c i) j -> p c j i", i=4),
        in_=src.rearrange("p j (c i) -> p c j i", i=4),
    )


def tile_routed_moe_kernel(tc, xT, w, b, gate, offs, pos1, pos2, out):
    nc = tc.nc
    with ExitStack() as ctx:
        lists = ctx.enter_context(tc.tile_pool(name="lists", bufs=1))
        keep = ctx.enter_context(tc.tile_pool(name="keep", bufs=1))
        psum = ctx.enter_context(tc.psum_pool(name="psum", bufs=1))

        xv = xT.rearrange("(p j) t -> p j t", j=PACK)
        xraw = {}
        t0 = 0
        for c, n in enumerate(XLOADS):
            r = keep.tile([P, PACK, n], F32, name="xraw%d" % c)
            nc.sync.dma_start(out=r[:], in_=xv[:, :, t0:t0 + n])
            for s0, m in XCOPIES:
                if t0 <= s0 < t0 + n:
                    xraw[s0] = r[:, :, s0 - t0:s0 - t0 + m]
            t0 += n
        offs_t = lists.tile([P, E * C // 16], U16, name="offs_t")
        nc.sync.dma_start(offs_t[:], offs)
        wraw = []
        for e in range(E):
            r = keep.tile([P, PACK, N], F32, name="wraw%d" % e, tag="wraw%d" % e, align_bytes=64)
            we = w[e].rearrange("(p j) n -> p j n", j=PACK)
            for n0 in range(0, N, N if e < E - 1 else P):
                n1 = n0 + (N if e < E - 1 else P)
                nc.sync.dma_start(out=r[:, :, n0:n1], in_=we[:, :, n0:n1])
            wraw.append(r)
        bt = keep.tile([P, H, E], F32, name="bt")
        nc.sync.dma_start(out=bt[:], in_=b.rearrange("(h p) e -> p h e", h=H))
        pos_t = []
        for r, lst in enumerate((pos1, pos2)):
            t = lists.tile([P, T // 16], U16, name="pos_t%d" % r)
            nc.sync.dma_start(t[:], lst)
            pos_t.append(t)
        gate_t = {}
        g = keep.tile([P, 2, T], F32, name="gate_t_0")
        nc.sync.dma_start(out=g[:], in_=gate[:, 0:P, :].rearrange("r p t -> p r t"))
        for r in range(2):
            gate_t[(r, 0)] = g[:, r, :]
        for r in range(2):
            g = keep.tile([P, T], F32, name="gate_t%d_1" % r)
            nc.sync.dma_start(out=g[:], in_=gate[r][P:2 * P, :])
            gate_t[(r, 1)] = g[:]

        warm = keep.tile([P, 1], F32, name="warm")
        warm2 = keep.tile([P, 1], F32, name="warm2")
        nc.vector.memset(warm[:], 0.0)
        nc.scalar.activation(out=warm2[:], in_=warm[:], func=GELU)

        xcodes = keep.tile([P, WINDOW], I32, name="xcodes", align_bytes=64)
        xscales = keep.tile([P, WINDOW], U8, name="xscales", align_bytes=64)
        nc.vector.memset(xcodes[:, T:WINDOW], 0)
        nc.gpsimd.memset(xscales[:], 0)
        ident = keep.tile([P, P], F32, name="ident")
        make_identity(nc, ident[:])
        xg = {}

        def xcopy(copy, s0, n, q0, m):
            if q0 not in xg:
                g = keep.tile([P, m, PACK], BF16, name="xg%d" % q0, align_bytes=64)
                xg[q0] = g
            interleave(copy, xg[q0][:, s0 - q0:s0 - q0 + n], xraw[s0])

        def xquant(q0, m):
            nc.vector.quantize_mx(
                out=xcodes[:, q0:q0 + m].bitcast(FP8X4),
                scales=xscales[:, q0:q0 + m],
                in_=xg[q0][:].rearrange("p t j -> p (t j)"),
            )

        xcopy(nc.vector.tensor_copy, 0, 256, 0, 256)
        xcopy(nc.scalar.copy, 256, 256, 256, 256)
        xquant(0, 256)
        xcopy(nc.vector.tensor_copy, 512, 256, 512, 256)
        xquant(256, 256)
        xcopy(nc.scalar.copy, 768, 128, 768, 128)
        xquant(512, 256)
        xcopy(nc.vector.tensor_copy, 896, 64, 896, 128)
        xcopy(nc.scalar.copy, 960, 64, 896, 128)
        xquant(768, 128)
        xquant(896, 128)

        wg = [keep.tile([P, E, P, PACK], BF16, name="wg%d" % h, align_bytes=64) for h in range(H)]

        def winterleave_half(copy, e, h):
            interleave(copy, wg[h][:, e], wraw[e][:, :, h * P:(h + 1) * P])

        for e in range(E):
            winterleave_half(nc.scalar.copy, e, 0)
        for e in range(E):
            winterleave_half(nc.scalar.copy, e, 1)

        gc, gs = [], []

        def gather_codes(i):
            s0, n = PIECES[i]
            c_ = keep.tile([P, n], U32, name="gc%d" % i, tag="wraw7" if i == 1 else "gc%d" % i, align_bytes=64)
            a = 0
            for m in CODE_CUTS[i]:
                window = xcodes[:] if m > C else xcodes[:, 0:T]
                nc.vector.tensor_copy(out=c_[:, a:a + m], in_=window.bitcast(U32).indirect(offs_t[:, (s0 + a) // 16:(s0 + a + m) // 16]))
                a += m
            gc.append(c_)

        def gather_scales(i):
            s0, n = PIECES[i]
            s_ = keep.tile([P, n], U8, name="gs%d" % i, tag="wraw4" if i == 1 else "gs%d" % i, align_bytes=64)
            nc.vector.tensor_copy(out=s_[:], in_=xscales[:].indirect(offs_t[:, s0 // 16:(s0 + n) // 16]))
            gs.append(s_)

        gather_codes(0)
        gather_scales(0)
        gather_scales(1)

        y = [keep.tile([P, E * C], F32, name="y%d" % h, tag="wraw6" if h == 0 else "y1", align_bytes=64) for h in range(H)]
        wc, ws = {}, {}

        banks = {}

        def sums(e, h):
            key, col = ((h, e // 2), e % 2) if e < 6 else ((e % 2, 3), h)
            if key not in banks:
                banks[key] = psum.tile([P, GS], F32, name="acc%d_%d" % key, tag="bank%d_%d" % key)
            return banks[key][:, col * C:(col + 1) * C]

        def products(i, h):
            cuts = []
            for e in (2 * i, 2 * i + 1):
                n = C // 2 if (e, h) == (E - 1, 0) else C
                cuts += [(e, c0, n) for c0 in range(0, C, n)]
            for e, c0, n in cuts:
                s0 = (e % 6) * C + c0
                nc.tensor.matmul_mx(
                    out=sums(e, h)[:, c0:c0 + n],
                    lhsT=wc[(h, e)].bitcast(FP8X4),
                    lhsT_scale=ws[(h, e)],
                    rhs=gc[e // 6][:, s0:s0 + n].bitcast(FP8X4),
                    rhs_scale=gs[e // 6][:, s0:s0 + n],
                    start=True,
                    stop=True,
                )
            for e, c0, n in cuts:
                nc.scalar.activation(
                    out=y[h][:, e * C + c0:e * C + c0 + n],
                    in_=sums(e, h)[:, c0:c0 + n],
                    func=GELU,
                    bias=bt[:, h, e:e + 1],
                )

        def wquant(h, e0, n):
            c_ = keep.tile([P, n * P], U32, name="wc%d_%d" % (h, e0), align_bytes=64)
            s_ = keep.tile([P, n * P], U8, name="ws%d_%d" % (h, e0), align_bytes=64)
            nc.vector.quantize_mx(
                out=c_[:].bitcast(FP8X4),
                scales=s_[:],
                in_=wg[h][:, e0:e0 + n].rearrange("p v n j -> p (v n j)"),
            )
            for v in range(n):
                wc[(h, e0 + v)] = c_[:, v * P:(v + 1) * P]
                ws[(h, e0 + v)] = s_[:, v * P:(v + 1) * P]

        wquant(0, 0, 4)
        products(0, 0)
        products(1, 0)
        wquant(0, 4, 4)
        products(2, 0)
        gather_codes(1)
        products(3, 0)
        wquant(1, 0, 8)
        for i in range(PAIRS):
            products(i, 1)

        def gathered_product(r, h, t0, n, name, tag):
            t = keep.tile([P, n], F32, name=name, tag=tag)
            nc.vector.tensor_tensor(
                out=t[:],
                in0=y[h][:].indirect(pos_t[r][:, t0 // 16:(t0 + n) // 16]),
                in1=gate_t[(r, h)][:, t0:t0 + n],
                op=MULT,
            )
            return t

        def store(queue, h, t0, n, tile_):
            queue.dma_start(out=out[h * P:(h + 1) * P, t0:t0 + n], in_=tile_[:])

        part = [gathered_product(r, 0, 0, T, "part%d_0" % r, "part%d_0" % r) for r in range(2)]
        first = gathered_product(0, 1, 0, T, "part0_1", "part0_1")
        second = gathered_product(1, 1, 0, T - LAST, "part1_1", "part1_1")

        o = keep.tile([P, PE_COLS], F32, name="o_pe")
        for k, a in enumerate(range(0, PE_COLS, 512)):
            b_ = min(a + 512, PE_COLS)
            total = psum.tile([P, b_ - a], F32, name="total%d" % k, tag="bank0_%d" % k)
            for r in range(2):
                nc.tensor.matmul(out=total[:], lhsT=ident[:], rhs=part[r][:, a:b_], start=(r == 0), stop=(r == 1))
            nc.scalar.copy(out=o[:, a:b_], in_=total[:])
        store(nc.scalar, 0, 0, PE_COLS, o)

        o = keep.tile([P, T - PE_COLS], F32, name="o_rest", tag="gate_t0_1")
        nc.vector.tensor_tensor(out=o[:], in0=part[0][:, PE_COLS:], in1=part[1][:, PE_COLS:], op=ADD)
        store(nc.sync, 0, PE_COLS, T - PE_COLS, o)

        o = keep.tile([P, T - LAST], F32, name="o_main")
        nc.vector.tensor_tensor(out=o[:], in0=first[:, 0:T - LAST], in1=second[:], op=ADD)
        store(nc.sync, 1, 0, T - LAST, o)

        second = gathered_product(1, 1, T - LAST, LAST, "part1_last", "part1_0")
        o = keep.tile([P, LAST], F32, name="o_last")
        nc.vector.tensor_tensor(out=o[:], in0=first[:, T - LAST:], in1=second[:], op=ADD)
        store(nc.sync, 1, T - LAST, LAST, o)
